import numpy as np
CORES = [5,13,29,37,53,69,77,101,133,141,157,165,181,197,205,229]
N = 16
TIMES = 2
def setup_inputs(rng):
    x = (rng.standard_normal((N, 128, 128), dtype=np.float32) / np.float32(np.sqrt(512 * N)))
    return {"x": x, "xt": x.transpose(0, 2, 1).copy()}
def setup_inputs_big(rng):
    d = setup_inputs(rng)
    for k in ("x", "xt"): d[k] = (d[k].astype(np.float32) * 1024.0).astype(d[k].dtype)
    return d
def setup_inputs_small(rng):
    d = setup_inputs(rng)
    for k in ("x", "xt"): d[k] = (d[k].astype(np.float32) * (1 / 1024.0)).astype(d[k].dtype)
    return d
def setup_inputs_apart(rng):
    d = setup_inputs(rng)
    f = (10.0 ** rng.permutation(np.linspace(-1.5, 1.5, N))).astype(np.float32).reshape(N, 1, 1)
    for k in ("x", "xt"): d[k] = (d[k].astype(np.float32) * f).astype(d[k].dtype)
    return d
def reference(x, xt):
    X = list(x.astype(np.float64))
    for _ in range(TIMES):
        G = sum(a.T @ a for a in X)
        X = [1.5 * a - 0.5 * (a @ G) for a in X]
    return {"y": np.stack(X).astype(np.float32)}

@@ -1,0 +1,169 @@
+from concourse.bass import DstId, RemoteDMATransfer
+from concourse.mybir import AluOpType
+
+N = 16
+K = 16
+W = 128 // K
+SCALE = 1.0 / 9.0
+D1, D2, D4 = -2.4375 * 9.0, 1.6875 * 81.0, 0.0625 * 6561.0
+
+F = "float32"
+SCRATCH = {
+    "xs": ("sbuf", [128, 128], F), "xts": ("sbuf", [128, 128], F),
+    "ks": ("sbuf", [128, 128], F), "k1": ("sbuf", [128, 128], F), "k2": ("sbuf", [128, 128], F),
+    "k4": ("sbuf", [128, 128], F), "kx": ("sbuf", [128, 128], F),
+    "a1": ("sbuf", [128, 128], F), "a2": ("sbuf", [128, 128], F), "a4": ("sbuf", [128, 128], F),
+    "xq": ("sbuf", [128, 128], F),
+    "gls": ("sbuf", [128, 128], F),
+    "s0": ("sbuf", [128, 128], F), "s1": ("sbuf", [128, 128], F),
+    "hs": ("sbuf", [128, 128], F), "h2s": ("sbuf", [128, 128], F), "bs": ("sbuf", [128, 128], F),
+    "zs": ("sbuf", [128, 128], F), "ys": ("sbuf", [128, 128], F),
+    "pg": ("psum", [128, 512], F), "ph": ("psum", [128, 512], F),
+    "pz": ("psum", [128, 512], F), "py": ("psum", [128, 512], F),
+    "gld": ("dram", [K, 128, W], F),
+    "land": ("dram", [N, 128, W], F),
+    "gd": ("dram", [2 * K, 128, W], F),
+}
+SEMAPHORES = ["ldx", "ldxt", "cm", "m0", "v0", "st", "sent", "landed", "arr0", "arr1", "d0", "d1",
+              "pa", "px", "vh", "mh", "v2", "vb", "mz", "v3", "my", "v4", "out"]
+
+
+def _chip(topo, c):
+    return (topo.host(c), topo.chip(c))
+
+
+def _plan(cores, topo):
+    def together(a, b):
+        return _chip(topo, a) == _chip(topo, b) or topo.same_plane(a, b)
+
+    planes = []
+    for c in cores:
+        for pl in planes:
+            if together(c, pl[0]):
+                pl.append(c)
+                break
+        else:
+            planes.append([c])
+    hosts = sorted({topo.host(c) for c in cores})
+    world = [h * topo.CORES_PER_HOST + i for h in hosts for i in range(topo.CORES_PER_HOST)]
+    dies = sorted({topo.die(c) for c in world})
+    owners = []
+    for pl in planes:
+        able = [c for c in world if c not in cores and together(c, pl[0])
+                and all(topo.may_write(c, d) for d in cores)]
+        chips = sorted({_chip(topo, c) for c in able})
+        chips = chips[::max(1, len(chips) // K)][:K]
+        mine = []
+        for j, ch in enumerate(chips):
+            here = [c for c in able if _chip(topo, c) == ch]
+            want = dies[j % len(dies)]
+            for prev in owners:
+                for o in prev:
+                    if topo.mates(here[0], o):
+                        want = [d for d in dies if d != topo.die(o)][0]
+            mine.append([c for c in here if topo.die(c) == want][0])
+        owners.append(mine)
+    return planes, owners
+
+
+def _engines(topo, src, dsts):
+    m = topo.mask(src, dsts[0])
+    for d in dsts:
+        m &= topo.mask(src, d)
+    return [1 << b for b in range(m.bit_length()) if (m >> b) & 1]
+
+
+def _dst(topo, d, src):
+    rid, pid = topo.addr(d, src)
+    return DstId(rid=rid, pnc=pid)
+
+
+def _owner(g, core, T, topo, p, k, planes):
+    S = T.sem
+    cores = list(T.cores)
+    dsts = cores[k % N:] + cores[:k % N]
+    eng = _engines(topo, core, dsts)
+    srcs = [T.land[i] for i in range(len(planes[p]))]
+    arr = S["arr%d" % p]
+    trs = []
+    for e, m in enumerate(eng):
+        to = dsts[e::len(eng)]
+        trs.append(RemoteDMATransfer(dst_ids=[_dst(topo, d, core) for d in to], dma_engine_mask=m, remote_sem=arr,
+                                     srcs=srcs, dsts=[T.gd[p * K + k] for _ in to], alu_op=1))
+    g.wait_ge(S.landed, len(srcs))
+    g.remote_dma_fused(trs, local_sem=S.sent)
+    g.wait_ge(S.sent, len(trs))
+
+
+def rank_program(g, core, T, topo):
+    planes, owners = _plan(list(T.cores), topo)
+    for p, own in enumerate(owners):
+        if core in own:
+            _owner(g, core, T, topo, p, own.index(core), planes)
+            return
+    if T.rank_of(core) is None:
+        return
+    S = T.sem
+    pe, ve, sy, sc = g.tensor, g.vector, g.sync, g.scalar
+    p = [core in pl for pl in planes].index(True)
+    i = planes[p].index(core)
+    C = slice(0, 128)
+
+    sy.dma_start(T.xs[:], T.x[:]).then_inc(S.ldx, 16)
+    sc.dma_start(T.xts[:], T.xt[:]).then_inc(S.ldxt, 16)
+    sy.wait_ge(S.v0, 1)
+    sy.dma_start(T.gld[:], T.gls[:]).then_inc(S.st, 16)
+    sy.wait_ge(S.arr0, K)
+    sy.dma_start(T.s0[:], T.gd[0:K]).then_inc(S.d0, 16)
+    sc.wait_ge(S.arr1, K)
+    sc.dma_start(T.s1[:], T.gd[K:2 * K]).then_inc(S.d1, 16)
+    sy.wait_ge(S.v4, 1)
+    sy.dma_start(T.y[:], T.ys[:]).then_inc(S.out, 16)
+    sy.wait_ge(S.out, 16)
+
+    own = owners[p]
+    eng = _engines(topo, core, own)
+    g.wait_ge(S.st, 16)
+    for lo in range(0, K, len(eng)):
+        trs = [RemoteDMATransfer(dst_ids=[_dst(topo, own[k], core)], dma_engine_mask=eng[k - lo], remote_sem=S.landed,
+                                 src=T.gld[k], dst=T.land[i])
+               for k in range(lo, min(K, lo + len(eng)))]
+        g.remote_dma_fused(trs, local_sem=S.sent)
+    g.wait_ge(S.sent, K)
+
+    pe.wait_ge(S.ldx, 16)
+    pe.matmul(T.pg[:, C], T.xs[:], T.xs[:], True, True).then_inc(S.m0, 1)
+    pe.wait_ge(S.vh, 1)
+    pe.matmul(T.ph[:, C], T.hs[:], T.hs[:], True, True).then_inc(S.mh, 1)
+    pe.wait_ge(S.pa, 3)
+    pe.matmul(T.py[:, C], T.a1[:], T.hs[:], True, False)
+    pe.wait_ge(S.v2, 1)
+    pe.matmul(T.pz[:, C], T.h2s[:], T.a4[:], True, True).then_inc(S.mz, 1)
+    pe.matmul(T.py[:, C], T.a2[:], T.h2s[:], False, False)
+    pe.wait_ge(S.v3, 1)
+    pe.wait_ge(S.vb, 1)
+    pe.matmul(T.py[:, C], T.zs[:], T.bs[:], False, True).then_inc(S.my, 1)
+
+    for t, v in ((T.ks, SCALE), (T.k1, D1), (T.k2, D2), (T.k4, D4), (T.kx, 2.25)):
+        ve.memset(t[:], v).then_inc(S.cm, 1)
+    ve.wait_ge(S.cm, 5)
+    ve.wait_ge(S.m0, 1)
+    ve.tensor_tensor(T.gls[:], T.pg[:, C], T.ks[:], AluOpType.mult).then_inc(S.v0, 1)
+    ve.wait_ge(S.ldxt, 16)
+    ve.tensor_tensor(T.a1[:], T.xts[:], T.k1[:], AluOpType.mult).then_inc(S.pa, 1)
+    ve.tensor_tensor(T.a2[:], T.xts[:], T.k2[:], AluOpType.mult).then_inc(S.pa, 1)
+    ve.tensor_tensor(T.a4[:], T.xts[:], T.k4[:], AluOpType.mult).then_inc(S.pa, 1)
+    ve.wait_ge(S.ldx, 16)
+    ve.tensor_tensor(T.xq[:], T.xs[:], T.kx[:], AluOpType.mult).then_inc(S.px, 1)
+    ve.wait_ge(S.d0, 16)
+    ve.wait_ge(S.d1, 16)
+    ve.tensor_tensor(T.hs[:], T.s0[:], T.s1[:], AluOpType.add).then_inc(S.vh, 1)
+    ve.wait_ge(S.mh, 1)
+    ve.tensor_copy(T.h2s[:], T.ph[:, C]).then_inc(S.v2, 1)
+    ve.wait_ge(S.vh, 1)
+    ve.tensor_tensor(T.bs[:], T.ph[:, C], T.hs[:], AluOpType.subtract).then_inc(S.vb, 1)
+    ve.wait_ge(S.mz, 1)
+    ve.tensor_copy(T.zs[:], T.pz[:, C]).then_inc(S.v3, 1)
+    ve.wait_ge(S.my, 1)
+    ve.wait_ge(S.px, 1)
+    ve.tensor_tensor(T.ys[:], T.py[:, C], T.xq[:], AluOpType.add).then_inc(S.v4, 1)

@@ -4,28 +4,36 @@ from concourse.mybir import AluOpType
 N = 16
 K = 16
 W = 128 // K
+HK = K // 2
+WI = W // 2
 SCALE = 1.0 / 9.0
-D1, D2, D4 = -2.4375 * 9.0, 1.6875 * 81.0, 0.0625 * 6561.0
+D1, D4 = -2.4375 * 9.0, 0.0625 * 6561.0
+A4 = -D1
+CI = 1.0 / 3.0 - A4 / D4
+RX = 2.25 - A4 * CI
 
 F = "float32"
 SCRATCH = {
     "xs": ("sbuf", [128, 128], F), "xts": ("sbuf", [128, 128], F),
-    "ks": ("sbuf", [128, 128], F), "k1": ("sbuf", [128, 128], F), "k2": ("sbuf", [128, 128], F),
-    "k4": ("sbuf", [128, 128], F), "kx": ("sbuf", [128, 128], F),
-    "a1": ("sbuf", [128, 128], F), "a2": ("sbuf", [128, 128], F), "a4": ("sbuf", [128, 128], F),
-    "xq": ("sbuf", [128, 128], F),
+    "ks": ("sbuf", [128, 128], F), "k4": ("sbuf", [128, 128], F), "k5": ("sbuf", [128, 128], F),
+    "kx": ("sbuf", [128, 128], F),
+    "idt": ("sbuf", [128, 129], F), "ci": ("sbuf", [128, 128], F),
+    "a4": ("sbuf", [128, 128], F), "a5": ("sbuf", [128, 128], F), "xq": ("sbuf", [128, 128], F),
     "gls": ("sbuf", [128, 128], F),
     "s0": ("sbuf", [128, 128], F), "s1": ("sbuf", [128, 128], F),
-    "hs": ("sbuf", [128, 128], F), "h2s": ("sbuf", [128, 128], F), "bs": ("sbuf", [128, 128], F),
-    "zs": ("sbuf", [128, 128], F), "ys": ("sbuf", [128, 128], F),
+    "hs": ("sbuf", [128, 128], F), "hm": ("sbuf", [128, 128], F), "h2s": ("sbuf", [128, 128], F),
+    "bs": ("sbuf", [128, 128], F), "ws": ("sbuf", [128, 128], F), "ys": ("sbuf", [128, 128], F),
     "pg": ("psum", [128, 512], F), "ph": ("psum", [128, 512], F),
     "pz": ("psum", [128, 512], F), "py": ("psum", [128, 512], F),
+    "idd": ("dram", [129 * 128 // WI, WI], F),
+    "idr": ("dram", [2 * K, 128, WI], F),
     "gld": ("dram", [K, 128, W], F),
     "land": ("dram", [N, 128, W], F),
     "gd": ("dram", [2 * K, 128, W], F),
 }
-SEMAPHORES = ["ldx", "ldxt", "cm", "m0", "v0", "st", "sent", "landed", "arr0", "arr1", "d0", "d1",
-              "pa", "px", "vh", "mh", "v2", "vb", "mz", "v3", "my", "v4", "out"]
+SEMAPHORES = ["ldx", "ldxt", "cm", "im", "i1", "i2", "ida", "m0", "v0", "st", "sent", "landed",
+              "arr00", "arr01", "arr10", "arr11", "d0", "d1",
+              "pa", "px", "vh", "vm", "mh", "v2", "vb", "mz", "v3", "my", "v4", "out"]
 
 
 def _chip(topo, c):
@@ -83,16 +91,24 @@ def _owner(g, core, T, topo, p, k, planes):
     cores = list(T.cores)
     dsts = cores[k % N:] + cores[:k % N]
     eng = _engines(topo, core, dsts)
+    j = p * K + k
+    g.vector.memset(T.idt[:, 0:1], CI).then_inc(S.im, 1)
+    g.vector.memset(T.idt[:, 1:129], 0.0).then_inc(S.im, 1)
+    g.sync.wait_ge(S.im, 2)
+    g.sync.dma_start(T.idd[:], T.idt[:]).then_inc(S.i1, 16)
+    g.wait_ge(S.i1, 16)
+    g.remote_dma_fused(
+        [RemoteDMATransfer(dst_ids=[_dst(topo, d, core) for d in dsts[e::len(eng)]], dma_engine_mask=m, remote_sem=S.ida,
+                           srcs=[T.idd[128 * j:128 * (j + 1), :]], dsts=[T.idr[j] for _ in dsts[e::len(eng)]])
+         for e, m in enumerate(eng)], local_sem=S.sent)
     srcs = [T.land[i] for i in range(len(planes[p]))]
-    arr = S["arr%d" % p]
-    trs = []
-    for e, m in enumerate(eng):
-        to = dsts[e::len(eng)]
-        trs.append(RemoteDMATransfer(dst_ids=[_dst(topo, d, core) for d in to], dma_engine_mask=m, remote_sem=arr,
-                                     srcs=srcs, dsts=[T.gd[p * K + k] for _ in to], alu_op=1))
+    arr = S["arr%d%d" % (p, k // HK)]
     g.wait_ge(S.landed, len(srcs))
-    g.remote_dma_fused(trs, local_sem=S.sent)
-    g.wait_ge(S.sent, len(trs))
+    g.remote_dma_fused(
+        [RemoteDMATransfer(dst_ids=[_dst(topo, d, core) for d in dsts[e::len(eng)]], dma_engine_mask=m, remote_sem=arr,
+                           srcs=srcs, dsts=[T.gd[j] for _ in dsts[e::len(eng)]], alu_op=1)
+         for e, m in enumerate(eng)], local_sem=S.sent)
+    g.wait_ge(S.sent, 2 * len(eng))
 
 
 def rank_program(g, core, T, topo):
@@ -110,16 +126,25 @@ def rank_program(g, core, T, topo):
     C = slice(0, 128)
 
     sy.dma_start(T.xs[:], T.x[:]).then_inc(S.ldx, 16)
-    sc.dma_start(T.xts[:], T.xt[:]).then_inc(S.ldxt, 16)
     sy.wait_ge(S.v0, 1)
     sy.dma_start(T.gld[:], T.gls[:]).then_inc(S.st, 16)
-    sy.wait_ge(S.arr0, K)
-    sy.dma_start(T.s0[:], T.gd[0:K]).then_inc(S.d0, 16)
-    sc.wait_ge(S.arr1, K)
-    sc.dma_start(T.s1[:], T.gd[K:2 * K]).then_inc(S.d1, 16)
+    sy.wait_ge(S.arr00, HK)
+    sy.dma_start(T.s0[0:64, :], T.gd[0:HK]).then_inc(S.d0, 16)
+    sy.wait_ge(S.arr01, HK)
+    sy.dma_start(T.s0[64:128, :], T.gd[HK:K]).then_inc(S.d0, 16)
     sy.wait_ge(S.v4, 1)
     sy.dma_start(T.y[:], T.ys[:]).then_inc(S.out, 16)
     sy.wait_ge(S.out, 16)
+
+    sc.wait_ge(S.ldx, 16)
+    sc.dma_start(T.xts[:], T.xt[:]).then_inc(S.ldxt, 16)
+    sc.wait_ge(S.sent, K)
+    sc.wait_ge(S.ida, 2 * K)
+    sc.dma_start(T.ci[:], T.idr[:]).then_inc(S.i2, 16)
+    sc.wait_ge(S.arr10, HK)
+    sc.dma_start(T.s1[0:64, :], T.gd[K:K + HK]).then_inc(S.d1, 16)
+    sc.wait_ge(S.arr11, HK)
+    sc.dma_start(T.s1[64:128, :], T.gd[K + HK:2 * K]).then_inc(S.d1, 16)
 
     own = owners[p]
     eng = _engines(topo, core, own)
@@ -135,35 +160,36 @@ def rank_program(g, core, T, topo):
     pe.matmul(T.pg[:, C], T.xs[:], T.xs[:], True, True).then_inc(S.m0, 1)
     pe.wait_ge(S.vh, 1)
     pe.matmul(T.ph[:, C], T.hs[:], T.hs[:], True, True).then_inc(S.mh, 1)
-    pe.wait_ge(S.pa, 3)
-    pe.matmul(T.py[:, C], T.a1[:], T.hs[:], True, False)
+    pe.wait_ge(S.pa, 2)
     pe.wait_ge(S.v2, 1)
     pe.matmul(T.pz[:, C], T.h2s[:], T.a4[:], True, True).then_inc(S.mz, 1)
-    pe.matmul(T.py[:, C], T.a2[:], T.h2s[:], False, False)
     pe.wait_ge(S.v3, 1)
     pe.wait_ge(S.vb, 1)
-    pe.matmul(T.py[:, C], T.zs[:], T.bs[:], False, True).then_inc(S.my, 1)
+    pe.matmul(T.py[:, C], T.ws[:], T.bs[:], True, True).then_inc(S.my, 1)
 
-    for t, v in ((T.ks, SCALE), (T.k1, D1), (T.k2, D2), (T.k4, D4), (T.kx, 2.25)):
+    for t, v in ((T.ks, SCALE), (T.k4, D4), (T.k5, A4), (T.kx, RX)):
         ve.memset(t[:], v).then_inc(S.cm, 1)
-    ve.wait_ge(S.cm, 5)
+    ve.wait_ge(S.cm, 4)
     ve.wait_ge(S.m0, 1)
     ve.tensor_tensor(T.gls[:], T.pg[:, C], T.ks[:], AluOpType.mult).then_inc(S.v0, 1)
-    ve.wait_ge(S.ldxt, 16)
-    ve.tensor_tensor(T.a1[:], T.xts[:], T.k1[:], AluOpType.mult).then_inc(S.pa, 1)
-    ve.tensor_tensor(T.a2[:], T.xts[:], T.k2[:], AluOpType.mult).then_inc(S.pa, 1)
-    ve.tensor_tensor(T.a4[:], T.xts[:], T.k4[:], AluOpType.mult).then_inc(S.pa, 1)
     ve.wait_ge(S.ldx, 16)
     ve.tensor_tensor(T.xq[:], T.xs[:], T.kx[:], AluOpType.mult).then_inc(S.px, 1)
-    ve.wait_ge(S.d0, 16)
-    ve.wait_ge(S.d1, 16)
+    ve.wait_ge(S.ldxt, 16)
+    ve.tensor_tensor(T.a4[:], T.xts[:], T.k4[:], AluOpType.mult).then_inc(S.pa, 1)
+    ve.tensor_tensor(T.a5[:], T.xts[:], T.k5[:], AluOpType.mult).then_inc(S.pa, 1)
+    ve.wait_ge(S.i2, 16)
+    ve.wait_ge(S.pa, 2)
+    ve.wait_ge(S.px, 1)
+    ve.wait_ge(S.d0, 32)
+    ve.wait_ge(S.d1, 32)
     ve.tensor_tensor(T.hs[:], T.s0[:], T.s1[:], AluOpType.add).then_inc(S.vh, 1)
+    ve.wait_ge(S.vh, 1)
+    ve.tensor_tensor(T.hm[:], T.hs[:], T.ci[:], AluOpType.subtract).then_inc(S.vm, 1)
     ve.wait_ge(S.mh, 1)
     ve.tensor_copy(T.h2s[:], T.ph[:, C]).then_inc(S.v2, 1)
-    ve.wait_ge(S.vh, 1)
-    ve.tensor_tensor(T.bs[:], T.ph[:, C], T.hs[:], AluOpType.subtract).then_inc(S.vb, 1)
+    ve.wait_ge(S.vm, 1)
+    ve.tensor_tensor(T.bs[:], T.ph[:, C], T.hm[:], AluOpType.subtract).then_inc(S.vb, 1)
     ve.wait_ge(S.mz, 1)
-    ve.tensor_copy(T.zs[:], T.pz[:, C]).then_inc(S.v3, 1)
+    ve.tensor_tensor(T.ws[:], T.pz[:, C], T.a5[:], AluOpType.add).then_inc(S.v3, 1)
     ve.wait_ge(S.my, 1)
-    ve.wait_ge(S.px, 1)
     ve.tensor_tensor(T.ys[:], T.py[:, C], T.xq[:], AluOpType.add).then_inc(S.v4, 1)

@@ -2,7 +2,7 @@ from concourse.bass import DstId, RemoteDMATransfer
 from concourse.mybir import AluOpType
 
 N = 16
-K = 16
+K = 32
 W = 128 // K
 HK = K // 2
 WI = W // 2
@@ -60,15 +60,10 @@ def _plan(cores, topo):
         able = [c for c in world if c not in cores and together(c, pl[0])
                 and all(topo.may_write(c, d) for d in cores)]
         chips = sorted({_chip(topo, c) for c in able})
-        chips = chips[::max(1, len(chips) // K)][:K]
         mine = []
-        for j, ch in enumerate(chips):
-            here = [c for c in able if _chip(topo, c) == ch]
-            want = dies[j % len(dies)]
-            for prev in owners:
-                for o in prev:
-                    if topo.mates(here[0], o):
-                        want = [d for d in dies if d != topo.die(o)][0]
+        for j in range(K):
+            here = [c for c in able if _chip(topo, c) == chips[j % len(chips)]]
+            want = dies[(j + j // len(chips)) % len(dies)]
             mine.append([c for c in here if topo.die(c) == want][0])
         owners.append(mine)
     return planes, owners

@@ -4,8 +4,12 @@ from concourse.mybir import AluOpType
 N = 16
 K = 32
 W = 128 // K
-HK = K // 2
-WI = W // 2
+Q = 4
+QK = K // Q
+RO = 96
+WO = RO // K
+NE = 8
+WN = (128 - RO) // NE
 SCALE = 1.0 / 9.0
 D1, D4 = -2.4375 * 9.0, 0.0625 * 6561.0
 A4 = -D1
@@ -23,17 +27,22 @@ SCRATCH = {
     "s0": ("sbuf", [128, 128], F), "s1": ("sbuf", [128, 128], F),
     "hs": ("sbuf", [128, 128], F), "hm": ("sbuf", [128, 128], F), "h2s": ("sbuf", [128, 128], F),
     "bs": ("sbuf", [128, 128], F), "ws": ("sbuf", [128, 128], F), "ys": ("sbuf", [128, 128], F),
-    "pg": ("psum", [128, 512], F), "ph": ("psum", [128, 512], F),
-    "pz": ("psum", [128, 512], F), "py": ("psum", [128, 512], F),
-    "idd": ("dram", [129 * 128 // WI, WI], F),
-    "idr": ("dram", [2 * K, 128, WI], F),
+    "pg0": ("psum", [128, 512], F), "pg1": ("psum", [128, 512], F),
+    "ph0": ("psum", [128, 512], F), "ph1": ("psum", [128, 512], F),
+    "pz0": ("psum", [128, 512], F), "pz1": ("psum", [128, 512], F),
+    "py0": ("psum", [128, 512], F), "py1": ("psum", [128, 512], F),
+    "idd": ("dram", [129 * 128 // WO, WO], F),
+    "idr": ("dram", [K, 128, WO], F),
+    "ids": ("dram", [129 * (128 - RO) // WN, WN], F),
+    "idn": ("dram", [NE, 128, WN], F),
     "gld": ("dram", [K, 128, W], F),
     "land": ("dram", [N, 128, W], F),
     "gd": ("dram", [2 * K, 128, W], F),
 }
-SEMAPHORES = ["ldx", "ldxt", "cm", "im", "i1", "i2", "ida", "m0", "v0", "st", "sent", "landed",
-              "arr00", "arr01", "arr10", "arr11", "d0", "d1",
-              "pa", "px", "vh", "vm", "mh", "v2", "vb", "mz", "v3", "my", "v4", "out"]
+SEMAPHORES = (["ldx", "ldxt", "cm", "im", "i1", "i2", "ida", "idb", "st", "sent", "landed", "d0", "d1",
+               "pa", "px", "vh", "vm", "out"]
+              + ["arr%d%d" % (p, q) for p in range(2) for q in range(Q)]
+              + [n + h for n in ("m0", "v0", "mh", "v2", "vb", "mz", "v3", "my", "v4") for h in "01"])
 
 
 def _chip(topo, c):
@@ -62,7 +71,7 @@ def _plan(cores, topo):
         chips = sorted({_chip(topo, c) for c in able})
         mine = []
         for j in range(K):
-            here = [c for c in able if _chip(topo, c) == chips[j % len(chips)]]
+            here = [c for c in able if _chip(topo, c) == chips[j % len(chips)] and c not in mine]
             want = dies[(j + j // len(chips)) % len(dies)]
             mine.append([c for c in here if topo.die(c) == want][0])
         owners.append(mine)
@@ -86,22 +95,23 @@ def _owner(g, core, T, topo, p, k, planes):
     cores = list(T.cores)
     dsts = cores[k % N:] + cores[:k % N]
     eng = _engines(topo, core, dsts)
-    j = p * K + k
+    half = cores[p * (N // 2):(p + 1) * (N // 2)]
+    half = half[k % len(half):] + half[:k % len(half)]
     g.vector.memset(T.idt[:, 0:1], CI).then_inc(S.im, 1)
     g.vector.memset(T.idt[:, 1:129], 0.0).then_inc(S.im, 1)
     g.sync.wait_ge(S.im, 2)
     g.sync.dma_start(T.idd[:], T.idt[:]).then_inc(S.i1, 16)
     g.wait_ge(S.i1, 16)
     g.remote_dma_fused(
-        [RemoteDMATransfer(dst_ids=[_dst(topo, d, core) for d in dsts[e::len(eng)]], dma_engine_mask=m, remote_sem=S.ida,
-                           srcs=[T.idd[128 * j:128 * (j + 1), :]], dsts=[T.idr[j] for _ in dsts[e::len(eng)]])
+        [RemoteDMATransfer(dst_ids=[_dst(topo, d, core) for d in half[e::len(eng)]], dma_engine_mask=m, remote_sem=S.ida,
+                           srcs=[T.idd[128 * k:128 * (k + 1), :]], dsts=[T.idr[k] for _ in half[e::len(eng)]])
          for e, m in enumerate(eng)], local_sem=S.sent)
     srcs = [T.land[i] for i in range(len(planes[p]))]
-    arr = S["arr%d%d" % (p, k // HK)]
+    arr = S["arr%d%d" % (p, k // QK)]
     g.wait_ge(S.landed, len(srcs))
     g.remote_dma_fused(
         [RemoteDMATransfer(dst_ids=[_dst(topo, d, core) for d in dsts[e::len(eng)]], dma_engine_mask=m, remote_sem=arr,
-                           srcs=srcs, dsts=[T.gd[j] for _ in dsts[e::len(eng)]], alu_op=1)
+                           srcs=srcs, dsts=[T.gd[p * K + k] for _ in dsts[e::len(eng)]], alu_op=1)
          for e, m in enumerate(eng)], local_sem=S.sent)
     g.wait_ge(S.sent, 2 * len(eng))
 
@@ -118,73 +128,99 @@ def rank_program(g, core, T, topo):
     pe, ve, sy, sc = g.tensor, g.vector, g.sync, g.scalar
     p = [core in pl for pl in planes].index(True)
     i = planes[p].index(core)
-    C = slice(0, 128)
+    HV = (slice(0, 64), slice(64, 128))
+    P0 = slice(0, 64)
+    R = 128 // Q
 
     sy.dma_start(T.xs[:], T.x[:]).then_inc(S.ldx, 16)
-    sy.wait_ge(S.v0, 1)
+    sy.wait_ge(S.v00, 1)
+    sy.wait_ge(S.v01, 1)
     sy.dma_start(T.gld[:], T.gls[:]).then_inc(S.st, 16)
-    sy.wait_ge(S.arr00, HK)
-    sy.dma_start(T.s0[0:64, :], T.gd[0:HK]).then_inc(S.d0, 16)
-    sy.wait_ge(S.arr01, HK)
-    sy.dma_start(T.s0[64:128, :], T.gd[HK:K]).then_inc(S.d0, 16)
-    sy.wait_ge(S.v4, 1)
+    for q in range(Q):
+        sy.wait_ge(S["arr0%d" % q], QK)
+        sy.dma_start(T.s0[R * q:R * (q + 1), :], T.gd[QK * q:QK * (q + 1)]).then_inc(S.d0, 16)
+    sy.wait_ge(S.v40, 1)
+    sy.wait_ge(S.v41, 1)
     sy.dma_start(T.y[:], T.ys[:]).then_inc(S.out, 16)
     sy.wait_ge(S.out, 16)
 
+    sc.wait_ge(S.im, 3)
+    sc.dma_start(T.ids[:], T.idt[0:128 - RO, :]).then_inc(S.i1, 16)
     sc.wait_ge(S.ldx, 16)
     sc.dma_start(T.xts[:], T.xt[:]).then_inc(S.ldxt, 16)
-    sc.wait_ge(S.sent, K)
-    sc.wait_ge(S.ida, 2 * K)
-    sc.dma_start(T.ci[:], T.idr[:]).then_inc(S.i2, 16)
-    sc.wait_ge(S.arr10, HK)
-    sc.dma_start(T.s1[0:64, :], T.gd[K:K + HK]).then_inc(S.d1, 16)
-    sc.wait_ge(S.arr11, HK)
-    sc.dma_start(T.s1[64:128, :], T.gd[K + HK:2 * K]).then_inc(S.d1, 16)
+    sc.wait_ge(S.sent, K + NE)
+    sc.wait_ge(S.ida, K)
+    sc.wait_ge(S.idb, NE)
+    sc.dma_start(T.ci[0:RO, :], T.idr[:]).then_inc(S.i2, 16)
+    sc.dma_start(T.ci[RO:128, :], T.idn[:]).then_inc(S.i2, 16)
+    for q in range(Q):
+        sc.wait_ge(S["arr1%d" % q], QK)
+        sc.dma_start(T.s1[R * q:R * (q + 1), :], T.gd[K + QK * q:K + QK * (q + 1)]).then_inc(S.d1, 16)
 
     own = owners[p]
     eng = _engines(topo, core, own)
+    nb = planes[p][(i + 1) % len(planes[p])]
+    g.wait_ge(S.i1, 16)
+    g.remote_dma_fused(
+        [RemoteDMATransfer(dst_ids=[_dst(topo, nb, core)], dma_engine_mask=m, remote_sem=S.idb,
+                           src=T.ids[128 * e:128 * (e + 1), :], dst=T.idn[e])
+         for e, m in enumerate(_engines(topo, core, [nb])[:NE])], local_sem=S.sent)
     g.wait_ge(S.st, 16)
     for lo in range(0, K, len(eng)):
         trs = [RemoteDMATransfer(dst_ids=[_dst(topo, own[k], core)], dma_engine_mask=eng[k - lo], remote_sem=S.landed,
                                  src=T.gld[k], dst=T.land[i])
                for k in range(lo, min(K, lo + len(eng)))]
         g.remote_dma_fused(trs, local_sem=S.sent)
-    g.wait_ge(S.sent, K)
+    g.wait_ge(S.sent, K + NE)
 
     pe.wait_ge(S.ldx, 16)
-    pe.matmul(T.pg[:, C], T.xs[:], T.xs[:], True, True).then_inc(S.m0, 1)
+    for h, c in enumerate(HV):
+        pe.matmul(T["pg%d" % h][:, P0], T.xs[:], T.xs[:, c], True, True).then_inc(S["m0%d" % h], 1)
     pe.wait_ge(S.vh, 1)
-    pe.matmul(T.ph[:, C], T.hs[:], T.hs[:], True, True).then_inc(S.mh, 1)
+    for h, c in enumerate(HV):
+        pe.matmul(T["ph%d" % h][:, P0], T.hs[:], T.hs[:, c], True, True).then_inc(S["mh%d" % h], 1)
     pe.wait_ge(S.pa, 2)
-    pe.wait_ge(S.v2, 1)
-    pe.matmul(T.pz[:, C], T.h2s[:], T.a4[:], True, True).then_inc(S.mz, 1)
-    pe.wait_ge(S.v3, 1)
-    pe.wait_ge(S.vb, 1)
-    pe.matmul(T.py[:, C], T.ws[:], T.bs[:], True, True).then_inc(S.my, 1)
+    pe.wait_ge(S.v20, 1)
+    pe.wait_ge(S.v21, 1)
+    for h, c in enumerate(HV):
+        pe.matmul(T["pz%d" % h][:, P0], T.h2s[:], T.a4[:, c], True, True).then_inc(S["mz%d" % h], 1)
+    pe.wait_ge(S.v30, 1)
+    pe.wait_ge(S.v31, 1)
+    for h, c in enumerate(HV):
+        pe.wait_ge(S["vb%d" % h], 1)
+        pe.matmul(T["py%d" % h][:, P0], T.ws[:], T.bs[:, c], True, True).then_inc(S["my%d" % h], 1)
 
+    ve.memset(T.idt[0:128 - RO, 0:RO], 0.0).then_inc(S.im, 1)
+    ve.memset(T.idt[0:128 - RO, RO:RO + 1], CI).then_inc(S.im, 1)
+    ve.memset(T.idt[0:128 - RO, RO + 1:129], 0.0).then_inc(S.im, 1)
     for t, v in ((T.ks, SCALE), (T.k4, D4), (T.k5, A4), (T.kx, RX)):
         ve.memset(t[:], v).then_inc(S.cm, 1)
     ve.wait_ge(S.cm, 4)
-    ve.wait_ge(S.m0, 1)
-    ve.tensor_tensor(T.gls[:], T.pg[:, C], T.ks[:], AluOpType.mult).then_inc(S.v0, 1)
+    for h, c in enumerate(HV):
+        ve.wait_ge(S["m0%d" % h], 1)
+        ve.tensor_tensor(T.gls[:, c], T["pg%d" % h][:, P0], T.ks[:, c], AluOpType.mult).then_inc(S["v0%d" % h], 1)
     ve.wait_ge(S.ldx, 16)
     ve.tensor_tensor(T.xq[:], T.xs[:], T.kx[:], AluOpType.mult).then_inc(S.px, 1)
     ve.wait_ge(S.ldxt, 16)
     ve.tensor_tensor(T.a4[:], T.xts[:], T.k4[:], AluOpType.mult).then_inc(S.pa, 1)
     ve.tensor_tensor(T.a5[:], T.xts[:], T.k5[:], AluOpType.mult).then_inc(S.pa, 1)
-    ve.wait_ge(S.i2, 16)
+    ve.wait_ge(S.i2, 32)
     ve.wait_ge(S.pa, 2)
     ve.wait_ge(S.px, 1)
-    ve.wait_ge(S.d0, 32)
-    ve.wait_ge(S.d1, 32)
+    ve.wait_ge(S.d0, 16 * Q)
+    ve.wait_ge(S.d1, 16 * Q)
     ve.tensor_tensor(T.hs[:], T.s0[:], T.s1[:], AluOpType.add).then_inc(S.vh, 1)
     ve.wait_ge(S.vh, 1)
     ve.tensor_tensor(T.hm[:], T.hs[:], T.ci[:], AluOpType.subtract).then_inc(S.vm, 1)
-    ve.wait_ge(S.mh, 1)
-    ve.tensor_copy(T.h2s[:], T.ph[:, C]).then_inc(S.v2, 1)
+    for h, c in enumerate(HV):
+        ve.wait_ge(S["mh%d" % h], 1)
+        ve.tensor_copy(T.h2s[:, c], T["ph%d" % h][:, P0]).then_inc(S["v2%d" % h], 1)
     ve.wait_ge(S.vm, 1)
-    ve.tensor_tensor(T.bs[:], T.ph[:, C], T.hm[:], AluOpType.subtract).then_inc(S.vb, 1)
-    ve.wait_ge(S.mz, 1)
-    ve.tensor_tensor(T.ws[:], T.pz[:, C], T.a5[:], AluOpType.add).then_inc(S.v3, 1)
-    ve.wait_ge(S.my, 1)
-    ve.tensor_tensor(T.ys[:], T.py[:, C], T.xq[:], AluOpType.add).then_inc(S.v4, 1)
+    for h, c in enumerate(HV):
+        ve.tensor_tensor(T.bs[:, c], T["ph%d" % h][:, P0], T.hm[:, c], AluOpType.subtract).then_inc(S["vb%d" % h], 1)
+    for h, c in enumerate(HV):
+        ve.wait_ge(S["mz%d" % h], 1)
+        ve.tensor_tensor(T.ws[:, c], T["pz%d" % h][:, P0], T.a5[:, c], AluOpType.add).then_inc(S["v3%d" % h], 1)
+    for h, c in enumerate(HV):
+        ve.wait_ge(S["my%d" % h], 1)
+        ve.tensor_tensor(T.ys[:, c], T["py%d" % h][:, P0], T.xq[:, c], AluOpType.add).then_inc(S["v4%d" % h], 1)

from concourse.bass import DstId, RemoteDMATransfer
from concourse.mybir import AluOpType

N = 16
K = 32
W = 128 // K
Q = 4
QK = K // Q
RO = 96
WO = RO // K
NE = 8
WN = (128 - RO) // NE
SCALE = 1.0 / 9.0
D1, D4 = -2.4375 * 9.0, 0.0625 * 6561.0
A4 = -D1
CI = 1.0 / 3.0 - A4 / D4
RX = 2.25 - A4 * CI

F = "float32"
SCRATCH = {
    "xs": ("sbuf", [128, 128], F), "xts": ("sbuf", [128, 128], F),
    "ks": ("sbuf", [128, 128], F), "k4": ("sbuf", [128, 128], F), "k5": ("sbuf", [128, 128], F),
    "kx": ("sbuf", [128, 128], F),
    "idt": ("sbuf", [128, 129], F), "ci": ("sbuf", [128, 128], F),
    "a4": ("sbuf", [128, 128], F), "a5": ("sbuf", [128, 128], F), "xq": ("sbuf", [128, 128], F),
    "gls": ("sbuf", [128, 128], F),
    "s0": ("sbuf", [128, 128], F), "s1": ("sbuf", [128, 128], F),
    "hs": ("sbuf", [128, 128], F), "hm": ("sbuf", [128, 128], F), "h2s": ("sbuf", [128, 128], F),
    "bs": ("sbuf", [128, 128], F), "ws": ("sbuf", [128, 128], F), "ys": ("sbuf", [128, 128], F),
    "pg0": ("psum", [128, 512], F), "pg1": ("psum", [128, 512], F),
    "ph0": ("psum", [128, 512], F), "ph1": ("psum", [128, 512], F),
    "pz0": ("psum", [128, 512], F), "pz1": ("psum", [128, 512], F),
    "py0": ("psum", [128, 512], F), "py1": ("psum", [128, 512], F),
    "idd": ("dram", [129 * 128 // WO, WO], F),
    "idr": ("dram", [K, 128, WO], F),
    "ids": ("dram", [129 * (128 - RO) // WN, WN], F),
    "idn": ("dram", [NE, 128, WN], F),
    "gld": ("dram", [K, 128, W], F),
    "land": ("dram", [N, 128, W], F),
    "gd": ("dram", [2 * K, 128, W], F),
}
SEMAPHORES = (["ldx", "ldxt", "cm", "im", "i1", "i2", "ida", "idb", "st", "sent", "landed", "d0", "d1",
               "pa", "px", "vh", "vm", "out"]
              + ["arr%d%d" % (p, q) for p in range(2) for q in range(Q)]
              + [n + h for n in ("m0", "v0", "mh", "v2", "vb", "mz", "v3", "my", "v4") for h in "01"])


def _chip(topo, c):
    return (topo.host(c), topo.chip(c))


def _plan(cores, topo):
    def together(a, b):
        return _chip(topo, a) == _chip(topo, b) or topo.same_plane(a, b)

    planes = []
    for c in cores:
        for pl in planes:
            if together(c, pl[0]):
                pl.append(c)
                break
        else:
            planes.append([c])
    hosts = sorted({topo.host(c) for c in cores})
    world = [h * topo.CORES_PER_HOST + i for h in hosts for i in range(topo.CORES_PER_HOST)]
    dies = sorted({topo.die(c) for c in world})
    owners = []
    for pl in planes:
        able = [c for c in world if c not in cores and together(c, pl[0])
                and all(topo.may_write(c, d) for d in cores)]
        chips = sorted({_chip(topo, c) for c in able})
        mine = []
        for j in range(K):
            here = [c for c in able if _chip(topo, c) == chips[j % len(chips)] and c not in mine]
            want = dies[(j + j // len(chips)) % len(dies)]
            mine.append([c for c in here if topo.die(c) == want][0])
        owners.append(mine)
    return planes, owners


def _engines(topo, src, dsts):
    m = topo.mask(src, dsts[0])
    for d in dsts:
        m &= topo.mask(src, d)
    return [1 << b for b in range(m.bit_length()) if (m >> b) & 1]


def _dst(topo, d, src):
    rid, pid = topo.addr(d, src)
    return DstId(rid=rid, pnc=pid)


def _owner(g, core, T, topo, p, k, planes):
    S = T.sem
    cores = list(T.cores)
    dsts = cores[k % N:] + cores[:k % N]
    eng = _engines(topo, core, dsts)
    half = cores[p * (N // 2):(p + 1) * (N // 2)]
    half = half[k % len(half):] + half[:k % len(half)]
    g.vector.memset(T.idt[:, 0:1], CI).then_inc(S.im, 1)
    g.vector.memset(T.idt[:, 1:129], 0.0).then_inc(S.im, 1)
    g.sync.wait_ge(S.im, 2)
    g.sync.dma_start(T.idd[:], T.idt[:]).then_inc(S.i1, 16)
    g.wait_ge(S.i1, 16)
    g.remote_dma_fused(
        [RemoteDMATransfer(dst_ids=[_dst(topo, d, core) for d in half[e::len(eng)]], dma_engine_mask=m, remote_sem=S.ida,
                           srcs=[T.idd[128 * k:128 * (k + 1), :]], dsts=[T.idr[k] for _ in half[e::len(eng)]])
         for e, m in enumerate(eng)], local_sem=S.sent)
    srcs = [T.land[i] for i in range(len(planes[p]))]
    arr = S["arr%d%d" % (p, k // QK)]
    g.wait_ge(S.landed, len(srcs))
    g.remote_dma_fused(
        [RemoteDMATransfer(dst_ids=[_dst(topo, d, core) for d in dsts[e::len(eng)]], dma_engine_mask=m, remote_sem=arr,
                           srcs=srcs, dsts=[T.gd[p * K + k] for _ in dsts[e::len(eng)]], alu_op=1)
         for e, m in enumerate(eng)], local_sem=S.sent)
    g.wait_ge(S.sent, 2 * len(eng))


def rank_program(g, core, T, topo):
    planes, owners = _plan(list(T.cores), topo)
    for p, own in enumerate(owners):
        if core in own:
            _owner(g, core, T, topo, p, own.index(core), planes)
            return
    if T.rank_of(core) is None:
        return
    S = T.sem
    pe, ve, sy, sc = g.tensor, g.vector, g.sync, g.scalar
    p = [core in pl for pl in planes].index(True)
    i = planes[p].index(core)
    HV = (slice(0, 64), slice(64, 128))
    P0 = slice(0, 64)
    R = 128 // Q

    sy.dma_start(T.xs[:], T.x[:]).then_inc(S.ldx, 16)
    sy.wait_ge(S.v00, 1)
    sy.wait_ge(S.v01, 1)
    sy.dma_start(T.gld[:], T.gls[:]).then_inc(S.st, 16)
    for q in range(Q):
        sy.wait_ge(S["arr0%d" % q], QK)
        sy.dma_start(T.s0[R * q:R * (q + 1), :], T.gd[QK * q:QK * (q + 1)]).then_inc(S.d0, 16)
    sy.wait_ge(S.v40, 1)
    sy.wait_ge(S.v41, 1)
    sy.dma_start(T.y[:], T.ys[:]).then_inc(S.out, 16)
    sy.wait_ge(S.out, 16)

    sc.wait_ge(S.im, 3)
    sc.dma_start(T.ids[:], T.idt[0:128 - RO, :]).then_inc(S.i1, 16)
    sc.wait_ge(S.ldx, 16)
    sc.dma_start(T.xts[:], T.xt[:]).then_inc(S.ldxt, 16)
    sc.wait_ge(S.sent, K + NE)
    sc.wait_ge(S.ida, K)
    sc.wait_ge(S.idb, NE)
    sc.dma_start(T.ci[0:RO, :], T.idr[:]).then_inc(S.i2, 16)
    sc.dma_start(T.ci[RO:128, :], T.idn[:]).then_inc(S.i2, 16)
    for q in range(Q):
        sc.wait_ge(S["arr1%d" % q], QK)
        sc.dma_start(T.s1[R * q:R * (q + 1), :], T.gd[K + QK * q:K + QK * (q + 1)]).then_inc(S.d1, 16)

    own = owners[p]
    eng = _engines(topo, core, own)
    nb = planes[p][(i + 1) % len(planes[p])]
    g.wait_ge(S.i1, 16)
    g.remote_dma_fused(
        [RemoteDMATransfer(dst_ids=[_dst(topo, nb, core)], dma_engine_mask=m, remote_sem=S.idb,
                           src=T.ids[128 * e:128 * (e + 1), :], dst=T.idn[e])
         for e, m in enumerate(_engines(topo, core, [nb])[:NE])], local_sem=S.sent)
    g.wait_ge(S.st, 16)
    for lo in range(0, K, len(eng)):
        trs = [RemoteDMATransfer(dst_ids=[_dst(topo, own[k], core)], dma_engine_mask=eng[k - lo], remote_sem=S.landed,
                                 src=T.gld[k], dst=T.land[i])
               for k in range(lo, min(K, lo + len(eng)))]
        g.remote_dma_fused(trs, local_sem=S.sent)
    g.wait_ge(S.sent, K + NE)

    pe.wait_ge(S.ldx, 16)
    for h, c in enumerate(HV):
        pe.matmul(T["pg%d" % h][:, P0], T.xs[:], T.xs[:, c], True, True).then_inc(S["m0%d" % h], 1)
    pe.wait_ge(S.vh, 1)
    for h, c in enumerate(HV):
        pe.matmul(T["ph%d" % h][:, P0], T.hs[:], T.hs[:, c], True, True).then_inc(S["mh%d" % h], 1)
    pe.wait_ge(S.pa, 2)
    pe.wait_ge(S.v20, 1)
    pe.wait_ge(S.v21, 1)
    for h, c in enumerate(HV):
        pe.matmul(T["pz%d" % h][:, P0], T.h2s[:], T.a4[:, c], True, True).then_inc(S["mz%d" % h], 1)
    pe.wait_ge(S.v30, 1)
    pe.wait_ge(S.v31, 1)
    for h, c in enumerate(HV):
        pe.wait_ge(S["vb%d" % h], 1)
        pe.matmul(T["py%d" % h][:, P0], T.ws[:], T.bs[:, c], True, True).then_inc(S["my%d" % h], 1)

    ve.memset(T.idt[0:128 - RO, 0:RO], 0.0).then_inc(S.im, 1)
    ve.memset(T.idt[0:128 - RO, RO:RO + 1], CI).then_inc(S.im, 1)
    ve.memset(T.idt[0:128 - RO, RO + 1:129], 0.0).then_inc(S.im, 1)
    for t, v in ((T.ks, SCALE), (T.k4, D4), (T.k5, A4), (T.kx, RX)):
        ve.memset(t[:], v).then_inc(S.cm, 1)
    ve.wait_ge(S.cm, 4)
    for h, c in enumerate(HV):
        ve.wait_ge(S["m0%d" % h], 1)
        ve.tensor_tensor(T.gls[:, c], T["pg%d" % h][:, P0], T.ks[:, c], AluOpType.mult).then_inc(S["v0%d" % h], 1)
    ve.wait_ge(S.ldx, 16)
    ve.tensor_tensor(T.xq[:], T.xs[:], T.kx[:], AluOpType.mult).then_inc(S.px, 1)
    ve.wait_ge(S.ldxt, 16)
    ve.tensor_tensor(T.a4[:], T.xts[:], T.k4[:], AluOpType.mult).then_inc(S.pa, 1)
    ve.tensor_tensor(T.a5[:], T.xts[:], T.k5[:], AluOpType.mult).then_inc(S.pa, 1)
    ve.wait_ge(S.i2, 32)
    ve.wait_ge(S.pa, 2)
    ve.wait_ge(S.px, 1)
    ve.wait_ge(S.d0, 16 * Q)
    ve.wait_ge(S.d1, 16 * Q)
    ve.tensor_tensor(T.hs[:], T.s0[:], T.s1[:], AluOpType.add).then_inc(S.vh, 1)
    ve.wait_ge(S.vh, 1)
    ve.tensor_tensor(T.hm[:], T.hs[:], T.ci[:], AluOpType.subtract).then_inc(S.vm, 1)
    for h, c in enumerate(HV):
        ve.wait_ge(S["mh%d" % h], 1)
        ve.tensor_copy(T.h2s[:, c], T["ph%d" % h][:, P0]).then_inc(S["v2%d" % h], 1)
    ve.wait_ge(S.vm, 1)
    for h, c in enumerate(HV):
        ve.tensor_tensor(T.bs[:, c], T["ph%d" % h][:, P0], T.hm[:, c], AluOpType.subtract).then_inc(S["vb%d" % h], 1)
    for h, c in enumerate(HV):
        ve.wait_ge(S["mz%d" % h], 1)
        ve.tensor_tensor(T.ws[:, c], T["pz%d" % h][:, P0], T.a5[:, c], AluOpType.add).then_inc(S["v3%d" % h], 1)
    for h, c in enumerate(HV):
        ve.wait_ge(S["my%d" % h], 1)
        ve.tensor_tensor(T.ys[:, c], T["py%d" % h][:, P0], T.xq[:, c], AluOpType.add).then_inc(S["v4%d" % h], 1)
